import numpy as np
import ml_dtypes


def mxq(x, axis, fmt="e4m3"):
    dtype, down = {"e4m3": (ml_dtypes.float8_e4m3fn, 7), "e5m2": (ml_dtypes.float8_e5m2, 14)}[fmt]
    v = np.moveaxis(np.asarray(x, np.float32).astype(ml_dtypes.bfloat16).astype(np.float64), axis, -1)
    blocks = v.reshape(v.shape[:-1] + (-1, 32))
    amax = np.abs(blocks).max(-1, keepdims=True)
    byte = np.maximum(np.where(amax > 0, np.frexp(amax)[1] - 1 + 127, 0) - down, 1)
    scale = np.exp2(byte - 127.0)
    codes = (blocks / scale).astype(np.float32).astype(dtype).astype(np.float64)
    return np.moveaxis((codes * scale).reshape(v.shape), -1, axis)


WIDE = False


def mx_kscale(k):
    if not WIDE:
        return np.ones(k)
    levels = np.array([10, -10, 5, -5, 0])
    if k % 512:
        return np.exp2(np.random.permutation(np.resize(levels, k // 32))).repeat(32)
    a = np.empty((k // 512, 16))
    for p in range(k // 512):
        a[p, :8] = np.random.permutation(np.resize(levels, 8))
        for g in range(8):
            far = levels[np.abs(levels - a[p, g]) >= 10]
            a[p, g + 8] = far[np.random.randint(len(far))]
    return np.exp2(a.ravel()).repeat(32)


def f64(x):
    return np.asarray(x).astype(np.float64)


def striped(idx):
    return np.tile(idx.reshape(-1, 16).T, (8, 1)).astype(np.uint16)


def unstriped(offs):
    return offs[:16].T.reshape(-1).astype(np.int64)


def striped8(idx):
    return np.concatenate([x.reshape(-1, 16).T for x in idx]).astype(np.uint16)


def runs(offs, k):
    lists = np.stack([offs[16 * r : 16 * r + 16].T.reshape(-1) for r in range(8)]).astype(np.int64)
    return lists[np.arange(k) % 512 // 64]


def pack_weight(w):
    k, n = w.shape
    w = f64(np.asarray(w, np.float32).astype(ml_dtypes.bfloat16)).reshape(k // 32, 32, n)
    amax = np.abs(w).max(1)
    byte = np.clip(np.where(amax > 0, np.frexp(amax)[1] - 1 + 127 - 7, 1), 1, 254)
    scaled = (w * np.exp2(127.0 - byte)[:, None, :]).reshape(k, n).astype(np.float32)
    words = np.ascontiguousarray(scaled.reshape(k // 512, 128, 4, n).transpose(0, 1, 3, 2)).astype(ml_dtypes.float8_e4m3fn).view(np.uint8)
    return words, np.ascontiguousarray(byte.astype(np.uint8).reshape(k // 512, 16, n))


def unpack_weight(words, scales):
    g, p, n, _ = words.shape
    vals = np.ascontiguousarray(words).view(ml_dtypes.float8_e4m3fn).astype(np.float64) * np.repeat(np.exp2(scales.astype(np.float64) - 127.0), 8, axis=1)[..., None]
    return vals.transpose(0, 1, 3, 2).reshape(g * 512, n)


K, T, S, N, G, H, W, U = 512, 1024, 256, 512, 2048, 512, 128, 1024


def setup_inputs():
    n = np.random.standard_normal
    s = mx_kscale(K)[:, None]
    u = mx_kscale(K)
    packed_xT = pack_weight(n((K, T)) * s)
    packed_dT = pack_weight(n((K, G)) / s)
    perm = np.random.permutation(S)
    return {
        "x_words": packed_xT[0],
        "x_scales": packed_xT[1],
        "d_words": packed_dT[0],
        "d_scales": packed_dT[1],
        "gn": (np.random.uniform(0.5, 1.5, (H, 1)) * u[:, None]).astype(np.float32),
        "w1": (n((H, N)) / np.sqrt(H) / u[:, None]).astype(np.float32),
        "offs": striped(np.random.permutation(T)[:S]),
        "ka": striped8(np.random.randint(0, G, (8, H))),
        "kb": striped8(np.random.randint(0, G, (8, H))),
        "n1": striped(perm[:W]),
        "n2": striped(perm[W:]),
        "n3": striped(np.random.permutation(U)[:S]),
        "n4": striped(np.random.permutation(S)),
    }


def reference(x_words, x_scales, d_words, d_scales, gn, w1, offs, ka, kb, n1, n2, n3, n4):
    d_ka = unpack_weight(d_words, d_scales)[np.arange(K)[:, None], runs(ka, K)]
    xq = unpack_weight(x_words, x_scales)[:, unstriped(offs)]
    d_kb = unpack_weight(d_words, d_scales)[np.arange(K)[:, None], runs(kb, K)]
    h = 0.0625 * (d_ka.T @ xq + d_kb.T @ xq)
    pb = h[:, unstriped(n2)]
    pa = h[:, unstriped(n1)]
    rb = pb - (0.5 * pa)
    ra = np.sqrt((pa) ** 2 + (pb) ** 2 + 0.25)
    ds = np.zeros((H, S))
    ds[:, unstriped(n1)] = ra
    dt = ds.copy()
    dt[:, unstriped(n2)] = rb
    z = f64(gn) * dt
    h2 = mxq(f64(w1), 0, "e4m3").T @ mxq(z, 0, "e4m3")
    nw = np.maximum(h2, h2[:, unstriped(n4)])
    out = np.zeros((N, U))
    out[:, unstriped(n3)] = nw
    return out

@@ -1,0 +1,223 @@
+from contextlib import ExitStack
+
+import concourse.mybir as mybir
+
+K, T, S, N, G, H, W, U = 512, 1024, 256, 512, 2048, 512, 128, 1024
+FLOPS = 2 * (2 * K * H * S) + 2 * H * N * S
+
+F32 = mybir.dt.float32
+BF16 = mybir.dt.bfloat16
+I32 = mybir.dt.int32
+U32 = mybir.dt.uint32
+U16 = mybir.dt.uint16
+U8 = mybir.dt.uint8
+FP8X4 = mybir.dt.float8_e4m3fn_x4
+ALU = mybir.AluOpType
+ACT = mybir.ActivationFunctionType
+
+P = 128
+PACK = 4
+TILES = 4
+
+
+def tile_picked_aqlpolarpags_none_p_kernel(
+    tc, x_words, x_scales, d_words, d_scales, gn, w1, offs, ka, kb, n1, n2, n3, n4, out
+):
+    nc = tc.nc
+    with ExitStack() as ctx:
+        lists = ctx.enter_context(tc.tile_pool(name="lists", bufs=1))
+        keep = ctx.enter_context(tc.tile_pool(name="keep", bufs=1))
+        psum = ctx.enter_context(tc.psum_pool(name="psum", bufs=1))
+
+        def load_list(src, name):
+            tile = lists.tile([P, src.shape[1]], U16, name=name)
+            nc.sync.dma_start(tile[:], src)
+            return tile
+
+        def load_scale_rows(src, cols, name):
+            tile = keep.tile([P, cols], U8, name=name)
+            rows = src[0].bitcast(I32)
+            nc.sync.dma_start(tile[:].bitcast(I32), rows.unsqueeze(1).to_broadcast([16, 8, cols // 4]))
+            return tile
+
+        def load_words(src, cols, name, tag):
+            tile = keep.tile([P, cols], U32, name=name, tag=tag)
+            nc.sync.dma_start(tile[:].bitcast(I32), src[0].rearrange("p n t -> p (n t)").bitcast(I32))
+            return tile
+
+        ds_table = load_scale_rows(d_scales, G, "ds_table")
+        ka_l = load_list(ka, "ka_l")
+        kb_l = load_list(kb, "kb_l")
+        xs_table = load_scale_rows(x_scales, T, "xs_table")
+        offs_l = load_list(offs, "offs_l")
+        xw_table = load_words(x_words, T, "xw_table", "xw_then_w1")
+        dw_table = load_words(d_words, G, "dw_table", "dw_table")
+        n1_l = load_list(n1, "n1_l")
+        n2_l = load_list(n2, "n2_l")
+        gains = keep.tile([P, TILES], F32, name="gains")
+        nc.sync.dma_start(gains[:], gn.rearrange("(p t) o -> p (t o)", t=TILES))
+        n4_l = load_list(n4, "n4_l")
+        n3_l = load_list(n3, "n3_l")
+
+        placed = keep.tile([P, 2 * H + S], U8, name="placed", align_bytes=64)
+        nc.vector.memset(placed[:].bitcast(I32), 0)
+        pages = [keep.tile([P, U], F32, name=f"page{t}") for t in range(TILES)]
+        nc.vector.memset(pages[0][:], 0.0)
+        for t in range(1, TILES):
+            nc.scalar.activation(out=pages[t][:], in_=pages[0][:], func=ACT.Copy)
+
+        picked_bytes = keep.tile([P, 2 * H + S], U8, name="picked_bytes")
+        nc.vector.tensor_copy(picked_bytes[:, 0:H], ds_table[:].indirect(ka_l[:]))
+        nc.vector.tensor_copy(picked_bytes[:, H : 2 * H], ds_table[:].indirect(kb_l[:]))
+        nc.vector.tensor_copy(picked_bytes[:, 2 * H :], xs_table[:].indirect(offs_l[:]))
+        for q in range(4):
+            nc.sync.dma_start(
+                placed[32 * q : 32 * q + 4, :].bitcast(I32),
+                picked_bytes[32 * q : 32 * q + 32 : 8, :].bitcast(I32),
+            )
+
+        x_codes = keep.tile([P, S], U32, name="x_codes", align_bytes=64)
+        nc.vector.tensor_copy(x_codes[:], xw_table[:].indirect(offs_l[:]))
+
+        w_raw = keep.tile([P, PACK, N], F32, name="w_raw", tag="xw_then_w1")
+        nc.sync.dma_start(w_raw[:], w1.rearrange("(p j) n -> p j n", j=PACK))
+
+        def deal_words(picked, name):
+            dealt = keep.tile([P, H], U32, name=name, align_bytes=64)
+            nc.vector.tensor_copy(
+                dealt[:].rearrange("p (t c i) -> p c t i", t=TILES, i=4),
+                picked[:].rearrange("p (c i t) -> p c t i", t=TILES, i=4),
+            )
+            return dealt
+
+        ka_picked = keep.tile([P, H], U32, name="ka_picked")
+        nc.vector.tensor_copy(ka_picked[:], dw_table[:].indirect(ka_l[:]))
+        kb_picked = keep.tile([P, H], U32, name="kb_picked")
+        nc.vector.tensor_copy(kb_picked[:], dw_table[:].indirect(kb_l[:]))
+        ka_codes = deal_words(ka_picked, "ka_codes")
+        d_planes = keep.tile([P, 2 * H], U8, name="d_planes", align_bytes=64)
+        nc.vector.tensor_copy(
+            d_planes[:].rearrange("p (t c i) -> p c t i", t=TILES, i=16),
+            placed[:, 0 : 2 * H].rearrange("p (c i t) -> p c t i", t=TILES, i=16),
+        )
+        kb_codes = deal_words(kb_picked, "kb_codes")
+
+        h_rows = []
+        for t in range(TILES):
+            acc = psum.tile([P, S], F32, name=f"h_acc{t}")
+            for a, codes in enumerate((ka_codes, kb_codes)):
+                nc.tensor.matmul_mx(
+                    out=acc[:],
+                    lhsT=codes[:, t * P : (t + 1) * P].bitcast(FP8X4),
+                    lhsT_scale=d_planes[:, (2 * t + a) * P : (2 * t + a + 1) * P],
+                    rhs=x_codes[:].bitcast(FP8X4),
+                    rhs_scale=placed[:, 2 * H :],
+                    start=(a == 0),
+                    stop=(a == 1),
+                )
+            h = keep.tile([P, S], F32, name=f"h{t}")
+            if t == 0:
+                nc.scalar.activation(out=h[:], in_=acc[:], func=ACT.Copy, scale=0.0625)
+            else:
+                nc.vector.tensor_scalar(h[:], acc[:], 0.0625, None, ALU.mult)
+            h_rows.append(h)
+
+        z_bf = keep.tile([P, S, TILES], BF16, name="z_bf", align_bytes=64)
+        w_codes = keep.tile([P, N], U32, name="w_codes", align_bytes=64)
+        w_planes = [keep.tile([P, P], U8, name=f"w_plane{t}", align_bytes=64) for t in range(TILES)]
+        pairs, rb, ra, dt = [], [], [], []
+
+        def fetch_pairs(t):
+            pab = keep.tile([P, 2, W], F32, name=f"pab{t}")
+            nc.scalar.activation(out=pab[:, 0, :], in_=h_rows[t][:].indirect(n1_l[:]), func=ACT.Copy)
+            nc.scalar.activation(out=pab[:, 1, :], in_=h_rows[t][:].indirect(n2_l[:]), func=ACT.Copy)
+            diff = keep.tile([P, W], F32, name=f"rb{t}")
+            nc.vector.scalar_tensor_tensor(diff[:], pab[:, 0, :], -0.5, pab[:, 1, :], ALU.mult, ALU.add)
+            squares = keep.tile([P, 2, W], F32, name=f"squares{t}", tag=f"squares_then_w{t}", align_bytes=64)
+            nc.vector.tensor_tensor(squares[:], pab[:], pab[:], ALU.mult)
+            radicand = keep.tile([P, W], F32, name=f"radicand{t}")
+            nc.vector.scalar_tensor_tensor(radicand[:], squares[:, 0, :], 0.25, squares[:, 1, :], ALU.add, ALU.add)
+            pairs.append(radicand)
+            rb.append(diff)
+            dt.append(keep.tile([P, S], F32, name=f"dt{t}"))
+
+        def quantise_w(t):
+            w_bf = keep.tile([P, P, PACK], BF16, name=f"w_bf{t}", tag=f"squares_then_w{t}", align_bytes=64)
+            nc.vector.tensor_copy(
+                w_bf[:].rearrange("p (c i) j -> p c j i", i=4),
+                w_raw[:, :, t * P : (t + 1) * P].rearrange("p j (c i) -> p c j i", i=4),
+            )
+            nc.vector.quantize_mx(
+                out=w_codes[:, t * P : (t + 1) * P].bitcast(FP8X4),
+                scales=w_planes[t][:],
+                in_=w_bf[:].rearrange("p m j -> p (m j)"),
+            )
+
+        def put_rb(t):
+            nc.scalar.activation(out=dt[t][:].indirect(n2_l[:]), in_=rb[t][:], func=ACT.Copy)
+
+        def root(t):
+            r = keep.tile([P, W], F32, name=f"ra{t}")
+            nc.scalar.activation(out=r[:], in_=pairs[t][:], func=ACT.Sqrt)
+            ra.append(r)
+
+        def put_ra(t):
+            nc.scalar.activation(out=dt[t][:].indirect(n1_l[:]), in_=ra[t][:], func=ACT.Copy)
+            nc.vector.tensor_scalar(z_bf[:, :, t], dt[t][:], gains[:, t : t + 1], None, ALU.mult)
+
+        fetch_pairs(0)
+        fetch_pairs(1)
+        for t in range(TILES):
+            put_rb(t)
+            if t > 0:
+                put_ra(t - 1)
+            root(t)
+            quantise_w(t)
+            if t + 2 < TILES:
+                fetch_pairs(t + 2)
+        put_ra(TILES - 1)
+
+        z_codes = keep.tile([P, S], U32, name="z_codes", align_bytes=64)
+        z_plane = keep.tile([P, S], U8, name="z_plane", align_bytes=64)
+        nc.vector.quantize_mx(out=z_codes[:].bitcast(FP8X4), scales=z_plane[:], in_=z_bf[:].rearrange("p s t -> p (s t)"))
+
+        larger = []
+
+        def second_product(t):
+            acc = psum.tile([P, S], F32, name=f"h2_acc{t}")
+            nc.tensor.matmul_mx(
+                out=acc[:],
+                lhsT=w_codes[:, t * P : (t + 1) * P].bitcast(FP8X4),
+                lhsT_scale=w_planes[t][:],
+                rhs=z_codes[:].bitcast(FP8X4),
+                rhs_scale=z_plane[:],
+                start=True,
+                stop=True,
+            )
+            h2 = keep.tile([P, S], F32, name=f"h2_{t}")
+            if t == 0:
+                nc.scalar.copy(h2[:], acc[:])
+            else:
+                nc.vector.tensor_copy(h2[:], acc[:])
+            return h2
+
+        h2_rows = [second_product(t) for t in range(TILES)]
+
+        def fetch_other(t):
+            other = keep.tile([P, S], F32, name=f"other{t}")
+            for half in range(2):
+                nc.scalar.activation(
+                    out=other[:, half * W : (half + 1) * W],
+                    in_=h2_rows[t][:].indirect(n4_l[:, half * 8 : (half + 1) * 8]),
+                    func=ACT.Copy,
+                )
+            nw = keep.tile([P, S], F32, name=f"nw{t}")
+            nc.vector.tensor_tensor(nw[:], h2_rows[t][:], other[:], ALU.max)
+            larger.append(nw)
+
+        fetch_other(0)
+        for t in range(TILES):
+            if t + 1 < TILES:
+                fetch_other(t + 1)
+            nc.scalar.activation(out=pages[t][:].indirect(n3_l[:]), in_=larger[t][:], func=ACT.Copy)
+            nc.sync.dma_start(out[t * P : (t + 1) * P, :], pages[t][:])

@@ -18,6 +18,7 @@ ACT = mybir.ActivationFunctionType
 P = 128
 PACK = 4
 TILES = 4
+RUN = 8
 
 
 def tile_picked_aqlpolarpags_none_p_kernel(
@@ -27,6 +28,7 @@ def tile_picked_aqlpolarpags_none_p_kernel(
     with ExitStack() as ctx:
         lists = ctx.enter_context(tc.tile_pool(name="lists", bufs=1))
         keep = ctx.enter_context(tc.tile_pool(name="keep", bufs=1))
+        shared = ctx.enter_context(tc.tile_pool(name="shared", bufs=1))
         psum = ctx.enter_context(tc.psum_pool(name="psum", bufs=1))
 
         def load_list(src, name):
@@ -34,28 +36,25 @@ def tile_picked_aqlpolarpags_none_p_kernel(
             nc.sync.dma_start(tile[:], src)
             return tile
 
-        def load_scale_rows(src, cols, name):
-            tile = keep.tile([P, cols], U8, name=name)
+        def load_scale_rows(src, cols, name, tag):
+            tile = keep.tile([P, cols], U8, name=name, tag=tag)
             rows = src[0].bitcast(I32)
-            nc.sync.dma_start(tile[:].bitcast(I32), rows.unsqueeze(1).to_broadcast([16, 8, cols // 4]))
+            nc.scalar.dma_start(tile[:].bitcast(I32), rows.unsqueeze(1).to_broadcast([16, 8, cols // 4]))
             return tile
 
-        def load_words(src, cols, name, tag):
-            tile = keep.tile([P, cols], U32, name=name, tag=tag)
+        def load_words(tile, src):
             nc.sync.dma_start(tile[:].bitcast(I32), src[0].rearrange("p n t -> p (n t)").bitcast(I32))
             return tile
 
-        ds_table = load_scale_rows(d_scales, G, "ds_table")
+        xs_table = load_scale_rows(x_scales, T, "xs_table", "xs_table")
+        offs_l = load_list(offs, "offs_l")
+        ds_table = load_scale_rows(d_scales, G, "ds_table", "ds_table")
         ka_l = load_list(ka, "ka_l")
         kb_l = load_list(kb, "kb_l")
-        xs_table = load_scale_rows(x_scales, T, "xs_table")
-        offs_l = load_list(offs, "offs_l")
-        xw_table = load_words(x_words, T, "xw_table", "xw_then_w1")
-        dw_table = load_words(d_words, G, "dw_table", "dw_table")
         n1_l = load_list(n1, "n1_l")
         n2_l = load_list(n2, "n2_l")
-        gains = keep.tile([P, TILES], F32, name="gains")
-        nc.sync.dma_start(gains[:], gn.rearrange("(p t) o -> p (t o)", t=TILES))
+        dw_table = load_words(keep.tile([P, G], U32, name="dw_table", tag="dw_then_w1"), d_words)
+        xw_table = load_words(shared.tile([P, T], U32, name="xw_table", offset=0, align_bytes=64), x_words)
         n4_l = load_list(n4, "n4_l")
         n3_l = load_list(n3, "n3_l")
 
@@ -64,52 +63,53 @@ def tile_picked_aqlpolarpags_none_p_kernel(
         pages = [keep.tile([P, U], F32, name=f"page{t}") for t in range(TILES)]
         nc.vector.memset(pages[0][:], 0.0)
         for t in range(1, TILES):
-            nc.scalar.activation(out=pages[t][:], in_=pages[0][:], func=ACT.Copy)
+            nc.scalar.activation(out=pages[t][:], in_=pages[0][:], func=ACT.Sqrt)
 
         picked_bytes = keep.tile([P, 2 * H + S], U8, name="picked_bytes")
+        nc.vector.tensor_copy(picked_bytes[:, 2 * H :], xs_table[:].indirect(offs_l[:]))
         nc.vector.tensor_copy(picked_bytes[:, 0:H], ds_table[:].indirect(ka_l[:]))
         nc.vector.tensor_copy(picked_bytes[:, H : 2 * H], ds_table[:].indirect(kb_l[:]))
-        nc.vector.tensor_copy(picked_bytes[:, 2 * H :], xs_table[:].indirect(offs_l[:]))
         for q in range(4):
             nc.sync.dma_start(
                 placed[32 * q : 32 * q + 4, :].bitcast(I32),
                 picked_bytes[32 * q : 32 * q + 32 : 8, :].bitcast(I32),
             )
 
+        picked_words = keep.tile([P, 2 * H], U32, name="picked_words")
+        nc.vector.tensor_copy(picked_words[:, 0:H], dw_table[:].indirect(ka_l[:]))
+        nc.vector.tensor_copy(picked_words[:, H:], dw_table[:].indirect(kb_l[:]))
+        w_raw = keep.tile([P, PACK, N], F32, name="w_raw", tag="dw_then_w1")
+        for j in range(PACK):
+            nc.sync.dma_start(w_raw[:, j, :], w1.rearrange("(b j e) n -> j b e n", j=PACK, e=RUN)[j])
+
         x_codes = keep.tile([P, S], U32, name="x_codes", align_bytes=64)
         nc.vector.tensor_copy(x_codes[:], xw_table[:].indirect(offs_l[:]))
 
-        w_raw = keep.tile([P, PACK, N], F32, name="w_raw", tag="xw_then_w1")
-        nc.sync.dma_start(w_raw[:], w1.rearrange("(p j) n -> p j n", j=PACK))
+        gains = []
+        for t in range(TILES):
+            gain = shared.tile([P, 1], F32, name=f"gain{t}", offset=2 * H + 64 * t, align_bytes=64)
+            with nc.allow_non_contiguous_dma(reason="one gain for each partition"):
+                nc.sync.dma_start(gain[:], gn.rearrange("(b t e) o -> t b e o", t=TILES, e=RUN)[t])
+            gains.append(gain)
 
-        def deal_words(picked, name):
-            dealt = keep.tile([P, H], U32, name=name, align_bytes=64)
-            nc.vector.tensor_copy(
-                dealt[:].rearrange("p (t c i) -> p c t i", t=TILES, i=4),
-                picked[:].rearrange("p (c i t) -> p c t i", t=TILES, i=4),
-            )
-            return dealt
-
-        ka_picked = keep.tile([P, H], U32, name="ka_picked")
-        nc.vector.tensor_copy(ka_picked[:], dw_table[:].indirect(ka_l[:]))
-        kb_picked = keep.tile([P, H], U32, name="kb_picked")
-        nc.vector.tensor_copy(kb_picked[:], dw_table[:].indirect(kb_l[:]))
-        ka_codes = deal_words(ka_picked, "ka_codes")
-        d_planes = keep.tile([P, 2 * H], U8, name="d_planes", align_bytes=64)
-        nc.vector.tensor_copy(
-            d_planes[:].rearrange("p (t c i) -> p c t i", t=TILES, i=16),
-            placed[:, 0 : 2 * H].rearrange("p (c i t) -> p c t i", t=TILES, i=16),
-        )
-        kb_codes = deal_words(kb_picked, "kb_codes")
-
+        d_planes = shared.tile([P, TILES, 2 * P], U8, name="d_planes", offset=0, align_bytes=64)
+        d_codes = shared.tile([P, TILES, 2 * P], U32, name="d_codes", offset=2 * H + 64 * TILES, align_bytes=64)
         h_rows = []
         for t in range(TILES):
-            acc = psum.tile([P, S], F32, name=f"h_acc{t}")
-            for a, codes in enumerate((ka_codes, kb_codes)):
+            nc.vector.tensor_copy(
+                d_codes[:, t, :].rearrange("p (c e) -> p c e", e=RUN),
+                picked_words[:].rearrange("p (c t e) -> p c t e", t=TILES, e=RUN)[:, :, t, :],
+            )
+            nc.vector.tensor_copy(
+                d_planes[:, t, :].bitcast(I32).rearrange("p (c e) -> p c e", e=RUN // 4),
+                placed[:, 0 : 2 * H].bitcast(I32).rearrange("p (c t e) -> p c t e", t=TILES, e=RUN // 4)[:, :, t, :],
+            )
+            acc = psum.tile([P, S], F32, name=f"h_acc{t}", tag=f"bank{t}")
+            for a in range(2):
                 nc.tensor.matmul_mx(
                     out=acc[:],
-                    lhsT=codes[:, t * P : (t + 1) * P].bitcast(FP8X4),
-                    lhsT_scale=d_planes[:, (2 * t + a) * P : (2 * t + a + 1) * P],
+                    lhsT=d_codes[:, t, a * P : (a + 1) * P].bitcast(FP8X4),
+                    lhsT_scale=d_planes[:, t, a * P : (a + 1) * P],
                     rhs=x_codes[:].bitcast(FP8X4),
                     rhs_scale=placed[:, 2 * H :],
                     start=(a == 0),
@@ -122,7 +122,7 @@ def tile_picked_aqlpolarpags_none_p_kernel(
                 nc.vector.tensor_scalar(h[:], acc[:], 0.0625, None, ALU.mult)
             h_rows.append(h)
 
-        z_bf = keep.tile([P, S, TILES], BF16, name="z_bf", align_bytes=64)
+        z_bf = [keep.tile([P, W, TILES], BF16, name=f"z_bf{half}", align_bytes=64) for half in range(2)]
         w_codes = keep.tile([P, N], U32, name="w_codes", align_bytes=64)
         w_planes = [keep.tile([P, P], U8, name=f"w_plane{t}", align_bytes=64) for t in range(TILES)]
         pairs, rb, ra, dt = [], [], [], []
@@ -163,7 +163,10 @@ def tile_picked_aqlpolarpags_none_p_kernel(
 
         def put_ra(t):
             nc.scalar.activation(out=dt[t][:].indirect(n1_l[:]), in_=ra[t][:], func=ACT.Copy)
-            nc.vector.tensor_scalar(z_bf[:, :, t], dt[t][:], gains[:, t : t + 1], None, ALU.mult)
+            for half in range(2):
+                nc.vector.tensor_scalar(
+                    z_bf[half][:, :, t], dt[t][:, half * W : (half + 1) * W], gains[t][:], None, ALU.mult
+                )
 
         fetch_pairs(0)
         fetch_pairs(1)
@@ -179,29 +182,33 @@ def tile_picked_aqlpolarpags_none_p_kernel(
 
         z_codes = keep.tile([P, S], U32, name="z_codes", align_bytes=64)
         z_plane = keep.tile([P, S], U8, name="z_plane", align_bytes=64)
-        nc.vector.quantize_mx(out=z_codes[:].bitcast(FP8X4), scales=z_plane[:], in_=z_bf[:].rearrange("p s t -> p (s t)"))
+        for half in range(2):
+            nc.vector.quantize_mx(
+                out=z_codes[:, half * W : (half + 1) * W].bitcast(FP8X4),
+                scales=z_plane[:, half * W : (half + 1) * W],
+                in_=z_bf[half][:].rearrange("p s t -> p (s t)"),
+            )
 
         larger = []
 
-        def second_product(t):
-            acc = psum.tile([P, S], F32, name=f"h2_acc{t}")
+        def second_product(t, cols, bank):
+            acc = psum.tile([P, cols.stop - cols.start], F32, name=f"h2_acc{bank}", tag=f"bank{bank}")
             nc.tensor.matmul_mx(
                 out=acc[:],
                 lhsT=w_codes[:, t * P : (t + 1) * P].bitcast(FP8X4),
                 lhsT_scale=w_planes[t][:],
-                rhs=z_codes[:].bitcast(FP8X4),
-                rhs_scale=z_plane[:],
+                rhs=z_codes[:, cols].bitcast(FP8X4),
+                rhs_scale=z_plane[:, cols],
                 start=True,
                 stop=True,
             )
-            h2 = keep.tile([P, S], F32, name=f"h2_{t}")
-            if t == 0:
-                nc.scalar.copy(h2[:], acc[:])
-            else:
-                nc.vector.tensor_copy(h2[:], acc[:])
-            return h2
+            return acc
 
-        h2_rows = [second_product(t) for t in range(TILES)]
+        h2_rows = [keep.tile([P, S], F32, name=f"h2_{t}") for t in range(TILES)]
+        nc.scalar.copy(h2_rows[0][:, 0:W], second_product(0, slice(0, W), 0)[:])
+        nc.vector.tensor_copy(h2_rows[0][:, W:], second_product(0, slice(W, S), 4)[:])
+        for t in range(1, TILES):
+            nc.vector.tensor_copy(h2_rows[t][:], second_product(t, slice(0, S), t)[:])
 
         def fetch_other(t):
             other = keep.tile([P, S], F32, name=f"other{t}")

@@ -65,6 +65,10 @@ def tile_picked_aqlpolarpags_none_p_kernel(
         for t in range(1, TILES):
             nc.scalar.activation(out=pages[t][:], in_=pages[0][:], func=ACT.Sqrt)
 
+        h2_rows = [keep.tile([P, S + 16], F32, name=f"h2_{t}") for t in range(TILES)]
+        for h2 in h2_rows:
+            nc.vector.memset(h2[:, S:], 0.0)
+
         picked_bytes = keep.tile([P, 2 * H + S], U8, name="picked_bytes")
         nc.vector.tensor_copy(picked_bytes[:, 2 * H :], xs_table[:].indirect(offs_l[:]))
         nc.vector.tensor_copy(picked_bytes[:, 0:H], ds_table[:].indirect(ka_l[:]))
@@ -125,7 +129,9 @@ def tile_picked_aqlpolarpags_none_p_kernel(
         z_bf = [keep.tile([P, W, TILES], BF16, name=f"z_bf{half}", align_bytes=64) for half in range(2)]
         w_codes = keep.tile([P, N], U32, name="w_codes", align_bytes=64)
         w_planes = [keep.tile([P, P], U8, name=f"w_plane{t}", align_bytes=64) for t in range(TILES)]
-        pairs, rb, ra, dt = [], [], [], []
+        rb, dt = [], []
+        radicand = keep.tile([P, TILES, W], F32, name="radicand")
+        ra = keep.tile([P, TILES, W], F32, name="ra")
 
         def fetch_pairs(t):
             pab = keep.tile([P, 2, W], F32, name=f"pab{t}")
@@ -135,9 +141,7 @@ def tile_picked_aqlpolarpags_none_p_kernel(
             nc.vector.scalar_tensor_tensor(diff[:], pab[:, 0, :], -0.5, pab[:, 1, :], ALU.mult, ALU.add)
             squares = keep.tile([P, 2, W], F32, name=f"squares{t}", tag=f"squares_then_w{t}", align_bytes=64)
             nc.vector.tensor_tensor(squares[:], pab[:], pab[:], ALU.mult)
-            radicand = keep.tile([P, W], F32, name=f"radicand{t}")
-            nc.vector.scalar_tensor_tensor(radicand[:], squares[:, 0, :], 0.25, squares[:, 1, :], ALU.add, ALU.add)
-            pairs.append(radicand)
+            nc.vector.scalar_tensor_tensor(radicand[:, t, :], squares[:, 0, :], 0.25, squares[:, 1, :], ALU.add, ALU.add)
             rb.append(diff)
             dt.append(keep.tile([P, S], F32, name=f"dt{t}"))
 
@@ -156,29 +160,24 @@ def tile_picked_aqlpolarpags_none_p_kernel(
         def put_rb(t):
             nc.scalar.activation(out=dt[t][:].indirect(n2_l[:]), in_=rb[t][:], func=ACT.Copy)
 
-        def root(t):
-            r = keep.tile([P, W], F32, name=f"ra{t}")
-            nc.scalar.activation(out=r[:], in_=pairs[t][:], func=ACT.Sqrt)
-            ra.append(r)
-
         def put_ra(t):
-            nc.scalar.activation(out=dt[t][:].indirect(n1_l[:]), in_=ra[t][:], func=ACT.Copy)
+            nc.scalar.activation(out=dt[t][:].indirect(n1_l[:]), in_=ra[:, t, :], func=ACT.Copy)
             for half in range(2):
                 nc.vector.tensor_scalar(
                     z_bf[half][:, :, t], dt[t][:, half * W : (half + 1) * W], gains[t][:], None, ALU.mult
                 )
 
-        fetch_pairs(0)
-        fetch_pairs(1)
         for t in range(TILES):
-            put_rb(t)
-            if t > 0:
-                put_ra(t - 1)
-            root(t)
+            fetch_pairs(t)
+        put_rb(0)
+        put_rb(1)
+        nc.scalar.activation(out=ra[:], in_=radicand[:], func=ACT.Sqrt)
+        put_rb(2)
+        put_rb(3)
+        for t in range(TILES):
             quantise_w(t)
-            if t + 2 < TILES:
-                fetch_pairs(t + 2)
-        put_ra(TILES - 1)
+        for t in range(TILES):
+            put_ra(t)
 
         z_codes = keep.tile([P, S], U32, name="z_codes", align_bytes=64)
         z_plane = keep.tile([P, S], U8, name="z_plane", align_bytes=64)
@@ -204,22 +203,16 @@ def tile_picked_aqlpolarpags_none_p_kernel(
             )
             return acc
 
-        h2_rows = [keep.tile([P, S], F32, name=f"h2_{t}") for t in range(TILES)]
         nc.scalar.copy(h2_rows[0][:, 0:W], second_product(0, slice(0, W), 0)[:])
-        nc.vector.tensor_copy(h2_rows[0][:, W:], second_product(0, slice(W, S), 4)[:])
+        nc.vector.tensor_copy(h2_rows[0][:, W:S], second_product(0, slice(W, S), 4)[:])
         for t in range(1, TILES):
-            nc.vector.tensor_copy(h2_rows[t][:], second_product(t, slice(0, S), t)[:])
+            nc.vector.tensor_copy(h2_rows[t][:, 0:S], second_product(t, slice(0, S), t)[:])
 
         def fetch_other(t):
             other = keep.tile([P, S], F32, name=f"other{t}")
-            for half in range(2):
-                nc.scalar.activation(
-                    out=other[:, half * W : (half + 1) * W],
-                    in_=h2_rows[t][:].indirect(n4_l[:, half * 8 : (half + 1) * 8]),
-                    func=ACT.Copy,
-                )
+            nc.scalar.activation(out=other[:], in_=h2_rows[t][:].indirect(n4_l[:]), func=ACT.Copy)
             nw = keep.tile([P, S], F32, name=f"nw{t}")
-            nc.vector.tensor_tensor(nw[:], h2_rows[t][:], other[:], ALU.max)
+            nc.vector.tensor_tensor(nw[:], h2_rows[t][:, 0:S], other[:], ALU.max)
             larger.append(nw)
 
         fetch_other(0)

@@ -96,35 +96,42 @@ def tile_picked_aqlpolarpags_none_p_kernel(
                 nc.sync.dma_start(gain[:], gn.rearrange("(b t e) o -> t b e o", t=TILES, e=RUN)[t])
             gains.append(gain)
 
-        d_planes = shared.tile([P, TILES, 2 * P], U8, name="d_planes", offset=0, align_bytes=64)
+        d_planes = [keep.tile([P, 2 * P], U8, name="d_plane0", align_bytes=64)] + [
+            shared.tile([P, 2 * P], U8, name=f"d_plane{t}", offset=2 * P * t, align_bytes=64) for t in range(1, TILES)
+        ]
         d_codes = shared.tile([P, TILES, 2 * P], U32, name="d_codes", offset=2 * H + 64 * TILES, align_bytes=64)
-        h_rows = []
-        for t in range(TILES):
-            nc.vector.tensor_copy(
-                d_codes[:, t, :].rearrange("p (c e) -> p c e", e=RUN),
-                picked_words[:].rearrange("p (c t e) -> p c t e", t=TILES, e=RUN)[:, :, t, :],
-            )
-            nc.vector.tensor_copy(
-                d_planes[:, t, :].bitcast(I32).rearrange("p (c e) -> p c e", e=RUN // 4),
-                placed[:, 0 : 2 * H].bitcast(I32).rearrange("p (c t e) -> p c t e", t=TILES, e=RUN // 4)[:, :, t, :],
-            )
-            acc = psum.tile([P, S], F32, name=f"h_acc{t}", tag=f"bank{t}")
+
+        def first_product(t, cols, bank):
+            acc = psum.tile([P, cols.stop - cols.start], F32, name=f"h_acc{bank}", tag=f"bank{bank}")
             for a in range(2):
                 nc.tensor.matmul_mx(
                     out=acc[:],
                     lhsT=d_codes[:, t, a * P : (a + 1) * P].bitcast(FP8X4),
-                    lhsT_scale=d_planes[:, t, a * P : (a + 1) * P],
-                    rhs=x_codes[:].bitcast(FP8X4),
-                    rhs_scale=placed[:, 2 * H :],
+                    lhsT_scale=d_planes[t][:, a * P : (a + 1) * P],
+                    rhs=x_codes[:, cols].bitcast(FP8X4),
+                    rhs_scale=placed[:, 2 * H + cols.start : 2 * H + cols.stop],
                     start=(a == 0),
                     stop=(a == 1),
                 )
-            h = keep.tile([P, S], F32, name=f"h{t}")
+            return acc
+
+        h_rows = [keep.tile([P, S], F32, name=f"h{t}") for t in range(TILES)]
+        for t in range(TILES):
+            nc.vector.tensor_copy(
+                d_planes[t][:].bitcast(I32).rearrange("p (c e) -> p c e", e=RUN // 4),
+                placed[:, 0 : 2 * H].bitcast(I32).rearrange("p (c t e) -> p c t e", t=TILES, e=RUN // 4)[:, :, t, :],
+            )
+            nc.vector.tensor_copy(
+                d_codes[:, t, :].rearrange("p (c e) -> p c e", e=RUN),
+                picked_words[:].rearrange("p (c t e) -> p c t e", t=TILES, e=RUN)[:, :, t, :],
+            )
             if t == 0:
-                nc.scalar.activation(out=h[:], in_=acc[:], func=ACT.Copy, scale=0.0625)
+                nc.scalar.activation(
+                    out=h_rows[0][:, 0:W], in_=first_product(0, slice(0, W), 0)[:], func=ACT.Copy, scale=0.0625
+                )
+                nc.vector.tensor_scalar(h_rows[0][:, W:], first_product(0, slice(W, S), 4)[:], 0.0625, None, ALU.mult)
             else:
-                nc.vector.tensor_scalar(h[:], acc[:], 0.0625, None, ALU.mult)
-            h_rows.append(h)
+                nc.vector.tensor_scalar(h_rows[t][:], first_product(t, slice(0, S), t)[:], 0.0625, None, ALU.mult)
 
         z_bf = [keep.tile([P, W, TILES], BF16, name=f"z_bf{half}", align_bytes=64) for half in range(2)]
         w_codes = keep.tile([P, N], U32, name="w_codes", align_bytes=64)

from contextlib import ExitStack

import concourse.mybir as mybir

K, T, S, N, G, H, W, U = 512, 1024, 256, 512, 2048, 512, 128, 1024
FLOPS = 2 * (2 * K * H * S) + 2 * H * N * S

F32 = mybir.dt.float32
BF16 = mybir.dt.bfloat16
I32 = mybir.dt.int32
U32 = mybir.dt.uint32
U16 = mybir.dt.uint16
U8 = mybir.dt.uint8
FP8X4 = mybir.dt.float8_e4m3fn_x4
ALU = mybir.AluOpType
ACT = mybir.ActivationFunctionType

P = 128
PACK = 4
TILES = 4
RUN = 8


def tile_picked_aqlpolarpags_none_p_kernel(
    tc, x_words, x_scales, d_words, d_scales, gn, w1, offs, ka, kb, n1, n2, n3, n4, out
):
    nc = tc.nc
    with ExitStack() as ctx:
        lists = ctx.enter_context(tc.tile_pool(name="lists", bufs=1))
        keep = ctx.enter_context(tc.tile_pool(name="keep", bufs=1))
        shared = ctx.enter_context(tc.tile_pool(name="shared", bufs=1))
        psum = ctx.enter_context(tc.psum_pool(name="psum", bufs=1))

        def load_list(src, name):
            tile = lists.tile([P, src.shape[1]], U16, name=name)
            nc.sync.dma_start(tile[:], src)
            return tile

        def load_scale_rows(src, cols, name, tag):
            tile = keep.tile([P, cols], U8, name=name, tag=tag)
            rows = src[0].bitcast(I32)
            nc.scalar.dma_start(tile[:].bitcast(I32), rows.unsqueeze(1).to_broadcast([16, 8, cols // 4]))
            return tile

        def load_words(tile, src):
            nc.sync.dma_start(tile[:].bitcast(I32), src[0].rearrange("p n t -> p (n t)").bitcast(I32))
            return tile

        xs_table = load_scale_rows(x_scales, T, "xs_table", "xs_table")
        offs_l = load_list(offs, "offs_l")
        ds_table = load_scale_rows(d_scales, G, "ds_table", "ds_table")
        ka_l = load_list(ka, "ka_l")
        kb_l = load_list(kb, "kb_l")
        n1_l = load_list(n1, "n1_l")
        n2_l = load_list(n2, "n2_l")
        dw_table = load_words(keep.tile([P, G], U32, name="dw_table", tag="dw_then_w1"), d_words)
        xw_table = load_words(shared.tile([P, T], U32, name="xw_table", offset=0, align_bytes=64), x_words)
        n4_l = load_list(n4, "n4_l")
        n3_l = load_list(n3, "n3_l")

        placed = keep.tile([P, 2 * H + S], U8, name="placed", align_bytes=64)
        nc.vector.memset(placed[:].bitcast(I32), 0)
        pages = [keep.tile([P, U], F32, name=f"page{t}") for t in range(TILES)]
        nc.vector.memset(pages[0][:], 0.0)
        for t in range(1, TILES):
            nc.scalar.activation(out=pages[t][:], in_=pages[0][:], func=ACT.Sqrt)

        h2_rows = [keep.tile([P, S + 16], F32, name=f"h2_{t}") for t in range(TILES)]
        for h2 in h2_rows:
            nc.vector.memset(h2[:, S:], 0.0)

        picked_bytes = keep.tile([P, 2 * H + S], U8, name="picked_bytes")
        nc.vector.tensor_copy(picked_bytes[:, 2 * H :], xs_table[:].indirect(offs_l[:]))
        nc.vector.tensor_copy(picked_bytes[:, 0:H], ds_table[:].indirect(ka_l[:]))
        nc.vector.tensor_copy(picked_bytes[:, H : 2 * H], ds_table[:].indirect(kb_l[:]))
        for q in range(4):
            nc.sync.dma_start(
                placed[32 * q : 32 * q + 4, :].bitcast(I32),
                picked_bytes[32 * q : 32 * q + 32 : 8, :].bitcast(I32),
            )

        picked_words = keep.tile([P, 2 * H], U32, name="picked_words")
        nc.vector.tensor_copy(picked_words[:, 0:H], dw_table[:].indirect(ka_l[:]))
        nc.vector.tensor_copy(picked_words[:, H:], dw_table[:].indirect(kb_l[:]))
        w_raw = keep.tile([P, PACK, N], F32, name="w_raw", tag="dw_then_w1")
        for j in range(PACK):
            nc.sync.dma_start(w_raw[:, j, :], w1.rearrange("(b j e) n -> j b e n", j=PACK, e=RUN)[j])

        x_codes = keep.tile([P, S], U32, name="x_codes", align_bytes=64)
        nc.vector.tensor_copy(x_codes[:], xw_table[:].indirect(offs_l[:]))

        gains = []
        for t in range(TILES):
            gain = shared.tile([P, 1], F32, name=f"gain{t}", offset=2 * H + 64 * t, align_bytes=64)
            with nc.allow_non_contiguous_dma(reason="one gain for each partition"):
                nc.sync.dma_start(gain[:], gn.rearrange("(b t e) o -> t b e o", t=TILES, e=RUN)[t])
            gains.append(gain)

        d_planes = [keep.tile([P, 2 * P], U8, name="d_plane0", align_bytes=64)] + [
            shared.tile([P, 2 * P], U8, name=f"d_plane{t}", offset=2 * P * t, align_bytes=64) for t in range(1, TILES)
        ]
        d_codes = shared.tile([P, TILES, 2 * P], U32, name="d_codes", offset=2 * H + 64 * TILES, align_bytes=64)

        def first_product(t, cols, bank):
            acc = psum.tile([P, cols.stop - cols.start], F32, name=f"h_acc{bank}", tag=f"bank{bank}")
            for a in range(2):
                nc.tensor.matmul_mx(
                    out=acc[:],
                    lhsT=d_codes[:, t, a * P : (a + 1) * P].bitcast(FP8X4),
                    lhsT_scale=d_planes[t][:, a * P : (a + 1) * P],
                    rhs=x_codes[:, cols].bitcast(FP8X4),
                    rhs_scale=placed[:, 2 * H + cols.start : 2 * H + cols.stop],
                    start=(a == 0),
                    stop=(a == 1),
                )
            return acc

        h_rows = [keep.tile([P, S], F32, name=f"h{t}") for t in range(TILES)]
        for t in range(TILES):
            nc.vector.tensor_copy(
                d_planes[t][:].bitcast(I32).rearrange("p (c e) -> p c e", e=RUN // 4),
                placed[:, 0 : 2 * H].bitcast(I32).rearrange("p (c t e) -> p c t e", t=TILES, e=RUN // 4)[:, :, t, :],
            )
            nc.vector.tensor_copy(
                d_codes[:, t, :].rearrange("p (c e) -> p c e", e=RUN),
                picked_words[:].rearrange("p (c t e) -> p c t e", t=TILES, e=RUN)[:, :, t, :],
            )
            if t == 0:
                nc.scalar.activation(
                    out=h_rows[0][:, 0:W], in_=first_product(0, slice(0, W), 0)[:], func=ACT.Copy, scale=0.0625
                )
                nc.vector.tensor_scalar(h_rows[0][:, W:], first_product(0, slice(W, S), 4)[:], 0.0625, None, ALU.mult)
            else:
                nc.vector.tensor_scalar(h_rows[t][:], first_product(t, slice(0, S), t)[:], 0.0625, None, ALU.mult)

        z_bf = [keep.tile([P, W, TILES], BF16, name=f"z_bf{half}", align_bytes=64) for half in range(2)]
        w_codes = keep.tile([P, N], U32, name="w_codes", align_bytes=64)
        w_planes = [keep.tile([P, P], U8, name=f"w_plane{t}", align_bytes=64) for t in range(TILES)]
        rb, dt = [], []
        radicand = keep.tile([P, TILES, W], F32, name="radicand")
        ra = keep.tile([P, TILES, W], F32, name="ra")

        def fetch_pairs(t):
            pab = keep.tile([P, 2, W], F32, name=f"pab{t}")
            nc.scalar.activation(out=pab[:, 0, :], in_=h_rows[t][:].indirect(n1_l[:]), func=ACT.Copy)
            nc.scalar.activation(out=pab[:, 1, :], in_=h_rows[t][:].indirect(n2_l[:]), func=ACT.Copy)
            diff = keep.tile([P, W], F32, name=f"rb{t}")
            nc.vector.scalar_tensor_tensor(diff[:], pab[:, 0, :], -0.5, pab[:, 1, :], ALU.mult, ALU.add)
            squares = keep.tile([P, 2, W], F32, name=f"squares{t}", tag=f"squares_then_w{t}", align_bytes=64)
            nc.vector.tensor_tensor(squares[:], pab[:], pab[:], ALU.mult)
            nc.vector.scalar_tensor_tensor(radicand[:, t, :], squares[:, 0, :], 0.25, squares[:, 1, :], ALU.add, ALU.add)
            rb.append(diff)
            dt.append(keep.tile([P, S], F32, name=f"dt{t}"))

        def quantise_w(t):
            w_bf = keep.tile([P, P, PACK], BF16, name=f"w_bf{t}", tag=f"squares_then_w{t}", align_bytes=64)
            nc.vector.tensor_copy(
                w_bf[:].rearrange("p (c i) j -> p c j i", i=4),
                w_raw[:, :, t * P : (t + 1) * P].rearrange("p j (c i) -> p c j i", i=4),
            )
            nc.vector.quantize_mx(
                out=w_codes[:, t * P : (t + 1) * P].bitcast(FP8X4),
                scales=w_planes[t][:],
                in_=w_bf[:].rearrange("p m j -> p (m j)"),
            )

        def put_rb(t):
            nc.scalar.activation(out=dt[t][:].indirect(n2_l[:]), in_=rb[t][:], func=ACT.Copy)

        def put_ra(t):
            nc.scalar.activation(out=dt[t][:].indirect(n1_l[:]), in_=ra[:, t, :], func=ACT.Copy)
            for half in range(2):
                nc.vector.tensor_scalar(
                    z_bf[half][:, :, t], dt[t][:, half * W : (half + 1) * W], gains[t][:], None, ALU.mult
                )

        for t in range(TILES):
            fetch_pairs(t)
        put_rb(0)
        put_rb(1)
        nc.scalar.activation(out=ra[:], in_=radicand[:], func=ACT.Sqrt)
        put_rb(2)
        put_rb(3)
        for t in range(TILES):
            quantise_w(t)
        for t in range(TILES):
            put_ra(t)

        z_codes = keep.tile([P, S], U32, name="z_codes", align_bytes=64)
        z_plane = keep.tile([P, S], U8, name="z_plane", align_bytes=64)
        for half in range(2):
            nc.vector.quantize_mx(
                out=z_codes[:, half * W : (half + 1) * W].bitcast(FP8X4),
                scales=z_plane[:, half * W : (half + 1) * W],
                in_=z_bf[half][:].rearrange("p s t -> p (s t)"),
            )

        larger = []

        def second_product(t, cols, bank):
            acc = psum.tile([P, cols.stop - cols.start], F32, name=f"h2_acc{bank}", tag=f"bank{bank}")
            nc.tensor.matmul_mx(
                out=acc[:],
                lhsT=w_codes[:, t * P : (t + 1) * P].bitcast(FP8X4),
                lhsT_scale=w_planes[t][:],
                rhs=z_codes[:, cols].bitcast(FP8X4),
                rhs_scale=z_plane[:, cols],
                start=True,
                stop=True,
            )
            return acc

        nc.scalar.copy(h2_rows[0][:, 0:W], second_product(0, slice(0, W), 0)[:])
        nc.vector.tensor_copy(h2_rows[0][:, W:S], second_product(0, slice(W, S), 4)[:])
        for t in range(1, TILES):
            nc.vector.tensor_copy(h2_rows[t][:, 0:S], second_product(t, slice(0, S), t)[:])

        def fetch_other(t):
            other = keep.tile([P, S], F32, name=f"other{t}")
            nc.scalar.activation(out=other[:], in_=h2_rows[t][:].indirect(n4_l[:]), func=ACT.Copy)
            nw = keep.tile([P, S], F32, name=f"nw{t}")
            nc.vector.tensor_tensor(nw[:], h2_rows[t][:, 0:S], other[:], ALU.max)
            larger.append(nw)

        fetch_other(0)
        for t in range(TILES):
            if t + 1 < TILES:
                fetch_other(t + 1)
            nc.scalar.activation(out=pages[t][:].indirect(n3_l[:]), in_=larger[t][:], func=ACT.Copy)
            nc.sync.dma_start(out[t * P : (t + 1) * P, :], pages[t][:])
